import numpy as np
import ml_dtypes


def mxq(x, axis, fmt="e4m3"):
    dtype, down = {"e4m3": (ml_dtypes.float8_e4m3fn, 7), "e5m2": (ml_dtypes.float8_e5m2, 14)}[fmt]
    v = np.moveaxis(np.asarray(x, np.float32).astype(ml_dtypes.bfloat16).astype(np.float64), axis, -1)
    blocks = v.reshape(v.shape[:-1] + (-1, 32))
    amax = np.abs(blocks).max(-1, keepdims=True)
    byte = np.maximum(np.where(amax > 0, np.frexp(amax)[1] - 1 + 127, 0) - down, 1)
    scale = np.exp2(byte - 127.0)
    codes = (blocks / scale).astype(np.float32).astype(dtype).astype(np.float64)
    return np.moveaxis((codes * scale).reshape(v.shape), -1, axis)


WIDE = False


def mx_kscale(k):
    if not WIDE:
        return np.ones(k)
    levels = np.array([10, -10, 5, -5, 0])
    if k % 512:
        return np.exp2(np.random.permutation(np.resize(levels, k // 32))).repeat(32)
    a = np.empty((k // 512, 16))
    for p in range(k // 512):
        a[p, :8] = np.random.permutation(np.resize(levels, 8))
        for g in range(8):
            far = levels[np.abs(levels - a[p, g]) >= 10]
            a[p, g + 8] = far[np.random.randint(len(far))]
    return np.exp2(a.ravel()).repeat(32)


def f64(x):
    return np.asarray(x).astype(np.float64)


def striped(idx):
    return np.tile(idx.reshape(-1, 16).T, (8, 1)).astype(np.uint16)


def unstriped(offs):
    return offs[:16].T.reshape(-1).astype(np.int64)


def striped8(idx):
    return np.concatenate([x.reshape(-1, 16).T for x in idx]).astype(np.uint16)


def runs(offs, k):
    lists = np.stack([offs[16 * r : 16 * r + 16].T.reshape(-1) for r in range(8)]).astype(np.int64)
    return lists[np.arange(k) % 512 // 64]


def pack_weight(w):
    k, n = w.shape
    w = f64(np.asarray(w, np.float32).astype(ml_dtypes.bfloat16)).reshape(k // 32, 32, n)
    amax = np.abs(w).max(1)
    byte = np.clip(np.where(amax > 0, np.frexp(amax)[1] - 1 + 127 - 7, 1), 1, 254)
    scaled = (w * np.exp2(127.0 - byte)[:, None, :]).reshape(k, n).astype(np.float32)
    words = np.ascontiguousarray(scaled.reshape(k // 512, 128, 4, n).transpose(0, 1, 3, 2)).astype(ml_dtypes.float8_e4m3fn).view(np.uint8)
    return words, np.ascontiguousarray(byte.astype(np.uint8).reshape(k // 512, 16, n))


def unpack_weight(words, scales):
    g, p, n, _ = words.shape
    vals = np.ascontiguousarray(words).view(ml_dtypes.float8_e4m3fn).astype(np.float64) * np.repeat(np.exp2(scales.astype(np.float64) - 127.0), 8, axis=1)[..., None]
    return vals.transpose(0, 1, 3, 2).reshape(g * 512, n)


K, T, S, N, H = 512, 2048, 512, 512, 512


def setup_inputs():
    n = np.random.standard_normal
    s = mx_kscale(K)[:, None]
    u = mx_kscale(H)
    packed_xT = pack_weight(n((K, T)) * s)
    return {
        "x_words": packed_xT[0],
        "x_scales": packed_xT[1],
        "w1": (n((K, H)) / np.sqrt(K) / s).astype(np.float32),
        "w2": (n((K, H)) / np.sqrt(K) / s).astype(np.float32),
        "gn": (np.random.uniform(0.5, 1.5, (H, 1)) * u[:, None]).astype(np.float32),
        "w3": (n((H, N)) / np.sqrt(H) / u[:, None]).astype(np.float32),
        "offs": striped(np.random.permutation(T)[:S]),
        "two": striped(np.random.permutation(T)[:S]),
        "e1": striped8(np.stack([np.random.permutation(S) for _ in range(8)])),
        "e0": striped8(np.stack([np.random.permutation(S) for _ in range(8)])),
        "v0": striped8(np.stack([np.random.permutation(S) for _ in range(8)])),
        "v1": striped8(np.stack([np.random.permutation(S) for _ in range(8)])),
    }


def reference(x_words, x_scales, w1, w2, gn, w3, offs, two, e1, e0, v0, v1):
    x_two = unpack_weight(x_words, x_scales)[:, unstriped(two)]
    c = mxq(f64(w2), 0, "e4m3").T @ x_two
    xq = unpack_weight(x_words, x_scales)[:, unstriped(offs)]
    y = mxq(f64(w1), 0, "e4m3").T @ xq
    t1 = np.clip(0.5 * (y[np.arange(H)[:, None], runs(e1, H)] - (y[np.arange(H)[:, None], runs(e0, H)])) + 0.5, 0.0, 1.0)
    sm = ((t1) ** 2) * (-2.0 * t1 + 3.0)
    z = f64(gn) * (c[np.arange(H)[:, None], runs(v0, H)] + sm * (c[np.arange(H)[:, None], runs(v1, H)] - (c[np.arange(H)[:, None], runs(v0, H)])))
    return mxq(f64(w3), 0, "e4m3").T @ mxq(z, 0, "e4m3")

@@ -1,0 +1,186 @@
+from contextlib import ExitStack
+
+import concourse.mybir as mybir
+
+K, T, S, N, H = 512, 2048, 512, 512, 512
+FLOPS = 3 * 2 * 512 * 512 * 512
+
+F32 = mybir.dt.float32
+BF16 = mybir.dt.bfloat16
+I32 = mybir.dt.int32
+U32 = mybir.dt.uint32
+U16 = mybir.dt.uint16
+U8 = mybir.dt.uint8
+FP8X4 = mybir.dt.float8_e4m3fn_x4
+ALU = mybir.AluOpType
+ACT = mybir.ActivationFunctionType
+
+P = 128
+PACK = 4
+HALF = 256
+CHUNKS = ((0, 256), (256, 128), (384, 128))
+
+
+def tile_picked_smstep_none_p_kernel(tc, x_words, x_scales, w1, w2, gn, w3, offs, two, e1, e0, v0, v1, out):
+    nc = tc.nc
+    with ExitStack() as ctx:
+        keep = ctx.enter_context(tc.tile_pool(name="keep", bufs=1))
+        psum = ctx.enter_context(tc.psum_pool(name="psum", bufs=1))
+
+        def load_list(name, src):
+            tile = keep.tile([P, S // 16], U16, name=name)
+            nc.sync.dma_start(tile[:], src)
+            return tile
+
+        def load_weight(name, w, c0=0, width=512):
+            raw = keep.tile([P, PACK, width], F32, name=name)
+            nc.sync.dma_start(out=raw[:], in_=w.rearrange("(p j) c -> p j c", j=PACK)[:, :, c0 : c0 + width])
+            return raw
+
+        def cast_weight(name, raws):
+            grouped = keep.tile([P, PACK * P * PACK], BF16, name=name, align_bytes=64)
+            dealt = grouped[:].rearrange("p (t m j) -> p m j t", t=PACK, j=PACK)
+            step = P // len(raws)
+            for i, raw in enumerate(raws):
+                nc.scalar.copy(out=dealt[:, i * step : (i + 1) * step], in_=raw[:].rearrange("p j (m t) -> p m j t", t=PACK))
+            return grouped
+
+        def quantize(name, grouped, width):
+            codes = keep.tile([P, width], U32, name=name + "_codes", align_bytes=64)
+            scales = keep.tile([P, width], U8, name=name + "_scales", align_bytes=64)
+            nc.vector.quantize_mx(out=codes[:].bitcast(FP8X4), scales=scales[:], in_=grouped)
+            return codes, scales
+
+        def product(acc, weight, t, moving):
+            cols = slice(t * P, (t + 1) * P)
+            nc.tensor.matmul_mx(
+                out=acc,
+                lhsT=weight[0][:, cols].bitcast(FP8X4),
+                lhsT_scale=weight[1][:, cols],
+                rhs=moving[0][:].bitcast(FP8X4),
+                rhs_scale=moving[1][:],
+                start=True,
+                stop=True,
+            )
+
+        xs = keep.tile([P, T], U8, name="xs", align_bytes=64)
+        nc.vector.memset(xs[:].bitcast(I32), 0)
+
+        offs_t = load_list("offs_t", offs)
+        two_t = load_list("two_t", two)
+        w1_raw = [load_weight("w1_raw0", w1, 0, 256)]
+        for q in range(4):
+            nc.sync.dma_start(out=xs[32 * q : 32 * q + 4, :].bitcast(I32), in_=x_scales[0][4 * q : 4 * q + 4, :].bitcast(I32))
+        w1_raw.append(load_weight("w1_raw1", w1, 256, 256))
+        xw = keep.tile([P, T], I32, name="xw", align_bytes=64)
+        nc.sync.dma_start(out=xw[:], in_=x_words[0].rearrange("p n t -> p (n t)").bitcast(I32))
+        e0_t = load_list("e0_t", e0)
+        e1_t = load_list("e1_t", e1)
+        w2_raw = load_weight("w2_raw", w2)
+        gain = keep.tile([P, PACK], F32, name="gain")
+        nc.sync.dma_start(out=gain[:], in_=gn.rearrange("(p t) o -> p (t o)", t=PACK))
+        v0_t = load_list("v0_t", v0)
+        v1_t = load_list("v1_t", v1)
+        w3_raw = load_weight("w3_raw", w3)
+
+        banks = [psum.tile([P, 512], F32, name="bank%d" % b) for b in range(8)]
+
+        def pick_scales(name, lst):
+            tile = keep.tile([P, S], U8, name=name, align_bytes=64)
+            nc.vector.tensor_copy(tile[:], xs[:].indirect(lst[:]))
+            return tile
+
+        def pick_words(name, lst):
+            tile = keep.tile([P, S], U32, name=name, align_bytes=64)
+            nc.vector.tensor_copy(tile[:], xw[:].bitcast(U32).indirect(lst[:]))
+            return tile
+
+        xq_scales = pick_scales("xq_scales", offs_t)
+        xt_scales = pick_scales("xt_scales", two_t)
+        w1_q = quantize("w1", cast_weight("w1_bf", w1_raw)[:], 512)
+        xq = (pick_words("xq_words", offs_t), xq_scales)
+        xt = (pick_words("xt_words", two_t), xt_scales)
+
+        y = []
+        for t in range(PACK):
+            product(banks[t][:], w1_q, t, xq)
+            tile = keep.tile([P, S], F32, name="y%d" % t)
+            nc.scalar.copy(out=tile[:], in_=banks[t][:])
+            y.append(tile)
+
+        low = keep.tile([P, PACK, S], F32, name="low")
+        diff = keep.tile([P, PACK, S], F32, name="diff")
+        clip = keep.tile([P, PACK, S], F32, name="clip")
+        square = keep.tile([P, PACK, S], F32, name="square")
+        stay = keep.tile([P, PACK, S], F32, name="stay")
+        move = keep.tile([P, PACK, S], F32, name="move")
+        part0 = keep.tile([P, PACK, S], F32, name="part0")
+        part1 = keep.tile([P, PACK, S], F32, name="part1")
+
+        def lists(lst, j0, n):
+            return lst[:, j0 // 16 : (j0 + n) // 16]
+
+        def fetch_y(h, t):
+            j0 = h * HALF
+            js = slice(j0, j0 + HALF)
+            nc.vector.tensor_copy(low[:, t, js], y[t][:].indirect(lists(e0_t, j0, HALF)))
+            nc.vector.tensor_tensor(diff[:, t, js], y[t][:].indirect(lists(e1_t, j0, HALF)), low[:, t, js], ALU.subtract)
+
+        def clamp(h, t):
+            js = slice(h * HALF, (h + 1) * HALF)
+            nc.vector.tensor_scalar(clip[:, t, js], diff[:, t, js], -1.0, 1.0, ALU.max, ALU.min)
+            nc.scalar.activation(square[:, t, js], clip[:, t, js], ACT.Square, bias=0.5, scale=-0.5)
+
+        def weights(h, t):
+            js = slice(h * HALF, (h + 1) * HALF)
+            nc.vector.scalar_tensor_tensor(stay[:, t, js], clip[:, t, js], 2.0, square[:, t, js], ALU.add, ALU.mult)
+            nc.scalar.activation(move[:, t, js], stay[:, t, js], ACT.Copy, bias=1.0, scale=-1.0)
+
+        units = [(h, t) for h in range(2) for t in range(PACK)]
+        c = []
+        for u in range(len(units) + 2):
+            if u < len(units):
+                fetch_y(*units[u])
+            if 1 <= u <= len(units):
+                clamp(*units[u - 1])
+            if u >= 2:
+                weights(*units[u - 2])
+            if u == 1:
+                w2_bf = cast_weight("w2_bf", [w2_raw])
+            if u == 3:
+                w2_q = quantize("w2", w2_bf[:], 512)
+                for t in range(PACK):
+                    product(banks[4 + t][:], w2_q, t, xt)
+                    tile = keep.tile([P, S], F32, name="c%d" % t)
+                    nc.scalar.activation(tile[:], banks[4 + t][:], ACT.Copy, scale=gain[:, t : t + 1])
+                    c.append(tile)
+            if u == 6:
+                w3_bf = cast_weight("w3_bf", [w3_raw])
+        w3_q = quantize("w3", w3_bf[:], 512)
+
+        out_rows = out.rearrange("(p t) j -> p t j", t=PACK)
+        bank = 0
+        for i, (j0, n) in enumerate(CHUNKS):
+            js = slice(j0, j0 + n)
+            for t in range(PACK):
+                nc.vector.tensor_tensor(part0[:, t, js], c[t][:].indirect(lists(v0_t, j0, n)), stay[:, t, js], ALU.mult)
+                nc.vector.tensor_tensor(part1[:, t, js], c[t][:].indirect(lists(v1_t, j0, n)), move[:, t, js], ALU.mult)
+            z = keep.tile([P, n * PACK], BF16, name="z%d" % i, align_bytes=64)
+            nc.vector.tensor_tensor(
+                z[:].rearrange("p (c i t) -> p c t i", i=4, t=PACK),
+                part0[:, :, js].rearrange("p t (c i) -> p c t i", i=4),
+                part1[:, :, js].rearrange("p t (c i) -> p c t i", i=4),
+                ALU.add,
+            )
+            z_q = quantize("z%d" % i, z[:], n)
+            res = keep.tile([P, PACK, n], F32, name="res%d" % i)
+            for t0 in range(0, PACK, 2):
+                for t in range(t0, t0 + 2):
+                    product(banks[bank][:, (t - t0) * n : (t - t0 + 1) * n], w3_q, t, z_q)
+                pair = res[:, t0 : t0 + 2, :].rearrange("p t j -> p (t j)")
+                if i == len(CHUNKS) - 1 and t0 == 2:
+                    nc.vector.tensor_copy(out=pair, in_=banks[bank][:, 0 : 2 * n])
+                else:
+                    nc.scalar.copy(out=pair, in_=banks[bank][:, 0 : 2 * n])
+                nc.sync.dma_start(out=out_rows[:, t0 : t0 + 2, js], in_=res[:, t0 : t0 + 2, :])
+                bank = bank + 1

@@ -1,6 +1,7 @@
 from contextlib import ExitStack
 
 import concourse.mybir as mybir
+from concourse.masks import make_identity
 
 K, T, S, N, H = 512, 2048, 512, 512, 512
 FLOPS = 3 * 2 * 512 * 512 * 512
@@ -33,12 +34,12 @@ def tile_picked_smstep_none_p_kernel(tc, x_words, x_scales, w1, w2, gn, w3, offs
             return tile
 
         def load_weight(name, w, c0=0, width=512):
-            raw = keep.tile([P, PACK, width], F32, name=name)
+            raw = keep.tile([P, PACK, width], F32, name=name, tag=name)
             nc.sync.dma_start(out=raw[:], in_=w.rearrange("(p j) c -> p j c", j=PACK)[:, :, c0 : c0 + width])
             return raw
 
-        def cast_weight(name, raws):
-            grouped = keep.tile([P, PACK * P * PACK], BF16, name=name, align_bytes=64)
+        def cast_weight(name, raws, tag):
+            grouped = keep.tile([P, PACK * P * PACK], BF16, name=name, tag=tag, align_bytes=64)
             dealt = grouped[:].rearrange("p (t m j) -> p m j t", t=PACK, j=PACK)
             step = P // len(raws)
             for i, raw in enumerate(raws):
@@ -51,14 +52,14 @@ def tile_picked_smstep_none_p_kernel(tc, x_words, x_scales, w1, w2, gn, w3, offs
             nc.vector.quantize_mx(out=codes[:].bitcast(FP8X4), scales=scales[:], in_=grouped)
             return codes, scales
 
-        def product(acc, weight, t, moving):
+        def product(acc, weight, t, moving, places=slice(None)):
             cols = slice(t * P, (t + 1) * P)
             nc.tensor.matmul_mx(
                 out=acc,
                 lhsT=weight[0][:, cols].bitcast(FP8X4),
                 lhsT_scale=weight[1][:, cols],
-                rhs=moving[0][:].bitcast(FP8X4),
-                rhs_scale=moving[1][:],
+                rhs=moving[0][:, places].bitcast(FP8X4),
+                rhs_scale=moving[1][:, places],
                 start=True,
                 stop=True,
             )
@@ -81,106 +82,187 @@ def tile_picked_smstep_none_p_kernel(tc, x_words, x_scales, w1, w2, gn, w3, offs
         nc.sync.dma_start(out=gain[:], in_=gn.rearrange("(p t) o -> p (t o)", t=PACK))
         v0_t = load_list("v0_t", v0)
         v1_t = load_list("v1_t", v1)
-        w3_raw = load_weight("w3_raw", w3)
+        w3_raw = [load_weight("w3_raw%d" % i, w3, 256 * i, 256) for i in range(2)]
 
         banks = [psum.tile([P, 512], F32, name="bank%d" % b) for b in range(8)]
+
+        def lists(lst, j0, n):
+            return lst[:, j0 // 16 : (j0 + n) // 16]
 
         def pick_scales(name, lst):
             tile = keep.tile([P, S], U8, name=name, align_bytes=64)
             nc.vector.tensor_copy(tile[:], xs[:].indirect(lst[:]))
             return tile
 
-        def pick_words(name, lst):
+        def pick_words(name, lst, n):
             tile = keep.tile([P, S], U32, name=name, align_bytes=64)
-            nc.vector.tensor_copy(tile[:], xw[:].bitcast(U32).indirect(lst[:]))
+            for j0 in range(0, S, n):
+                nc.vector.tensor_copy(tile[:, j0 : j0 + n], xw[:].bitcast(U32).indirect(lists(lst, j0, n)))
             return tile
 
         xq_scales = pick_scales("xq_scales", offs_t)
         xt_scales = pick_scales("xt_scales", two_t)
-        w1_q = quantize("w1", cast_weight("w1_bf", w1_raw)[:], 512)
-        xq = (pick_words("xq_words", offs_t), xq_scales)
-        xt = (pick_words("xt_words", two_t), xt_scales)
+        w1_q = quantize("w1", cast_weight("w1_bf", w1_raw, "w1_bf")[:], 512)
+        xq = (pick_words("xq_words", offs_t, HALF), xq_scales)
+        xt = (pick_words("xt_words", two_t, S), xt_scales)
 
-        y = []
-        for t in range(PACK):
-            product(banks[t][:], w1_q, t, xq)
-            tile = keep.tile([P, S], F32, name="y%d" % t)
-            nc.scalar.copy(out=tile[:], in_=banks[t][:])
-            y.append(tile)
+        ident = keep.tile([P, P], F32, name="ident")
+        make_identity(nc, ident[:])
 
-        low = keep.tile([P, PACK, S], F32, name="low")
+        early_low = keep.tile([P, 2, S], F32, name="early_low")
         diff = keep.tile([P, PACK, S], F32, name="diff")
         clip = keep.tile([P, PACK, S], F32, name="clip")
         square = keep.tile([P, PACK, S], F32, name="square")
         stay = keep.tile([P, PACK, S], F32, name="stay")
         move = keep.tile([P, PACK, S], F32, name="move")
-        part0 = keep.tile([P, PACK, S], F32, name="part0")
-        part1 = keep.tile([P, PACK, S], F32, name="part1")
+        part0 = keep.tile([P, PACK, HALF], F32, name="part0")
+        part1 = keep.tile([P, PACK, HALF], F32, name="part1")
 
-        def lists(lst, j0, n):
-            return lst[:, j0 // 16 : (j0 + n) // 16]
+        def fetch_y(tiles, low):
+            for t in tiles:
+                nc.vector.tensor_copy(low[:, t % 2, :], y[t][:].indirect(e0_t[:]))
+            for t in tiles:
+                nc.vector.tensor_tensor(diff[:, t, :], y[t][:].indirect(e1_t[:]), low[:, t % 2, :], ALU.subtract)
 
-        def fetch_y(h, t):
-            j0 = h * HALF
-            js = slice(j0, j0 + HALF)
-            nc.vector.tensor_copy(low[:, t, js], y[t][:].indirect(lists(e0_t, j0, HALF)))
-            nc.vector.tensor_tensor(diff[:, t, js], y[t][:].indirect(lists(e1_t, j0, HALF)), low[:, t, js], ALU.subtract)
+        def raise_floor(t):
+            nc.scalar.activation(above[:, t % 2, :], diff[:, t, :], ACT.Relu, bias=1.0, scale=-1.0)
 
-        def clamp(h, t):
-            js = slice(h * HALF, (h + 1) * HALF)
-            nc.vector.tensor_scalar(clip[:, t, js], diff[:, t, js], -1.0, 1.0, ALU.max, ALU.min)
-            nc.scalar.activation(square[:, t, js], clip[:, t, js], ACT.Square, bias=0.5, scale=-0.5)
+        def lower_ceiling(t):
+            nc.scalar.activation(clip[:, t, :], above[:, t % 2, :], ACT.Relu, bias=2.0, scale=-1.0)
 
-        def weights(h, t):
-            js = slice(h * HALF, (h + 1) * HALF)
-            nc.vector.scalar_tensor_tensor(stay[:, t, js], clip[:, t, js], 2.0, square[:, t, js], ALU.add, ALU.mult)
-            nc.scalar.activation(move[:, t, js], stay[:, t, js], ACT.Copy, bias=1.0, scale=-1.0)
+        def squared(t):
+            nc.scalar.activation(square[:, t, :], clip[:, t, :], ACT.Square, bias=1.0, scale=-0.5)
 
-        units = [(h, t) for h in range(2) for t in range(PACK)]
-        c = []
-        for u in range(len(units) + 2):
-            if u < len(units):
-                fetch_y(*units[u])
-            if 1 <= u <= len(units):
-                clamp(*units[u - 1])
-            if u >= 2:
-                weights(*units[u - 2])
-            if u == 1:
-                w2_bf = cast_weight("w2_bf", [w2_raw])
-            if u == 3:
-                w2_q = quantize("w2", w2_bf[:], 512)
-                for t in range(PACK):
-                    product(banks[4 + t][:], w2_q, t, xt)
-                    tile = keep.tile([P, S], F32, name="c%d" % t)
-                    nc.scalar.activation(tile[:], banks[4 + t][:], ACT.Copy, scale=gain[:, t : t + 1])
-                    c.append(tile)
-            if u == 6:
-                w3_bf = cast_weight("w3_bf", [w3_raw])
-        w3_q = quantize("w3", w3_bf[:], 512)
+        def stay_weight(ts):
+            nc.vector.scalar_tensor_tensor(stay[:, ts, :], clip[:, ts, :], 1.0, square[:, ts, :], ALU.add, ALU.mult)
+
+        def move_weight(ts):
+            nc.scalar.activation(move[:, ts, :], stay[:, ts, :], ACT.Copy, bias=1.0, scale=-1.0)
+
+        y = []
+        for t in range(PACK):
+            tile = keep.tile([P, 2 * S], F32, name="y%d" % t)
+            y.append(tile)
+        for h in range(2):
+            places = slice(h * HALF, (h + 1) * HALF)
+            for t in range(2):
+                bank = banks[4 * h + t]
+                product(bank[:, 0:HALF], w1_q, t, xq, places)
+                nc.scalar.copy(out=y[t][:, places], in_=bank[:, 0:HALF])
+        for t in range(2, PACK):
+            product(banks[t][:], w1_q, t, xq)
+            nc.scalar.copy(out=y[t][:, 0:S], in_=banks[t][:])
+        w2_q = quantize("w2", cast_weight("w2_bf", [w2_raw], "w2_bf")[:], 512)
+
+        late_low = keep.tile([P, 2, S], F32, name="late_low", tag="w2_bf", align_bytes=64)
+        above = keep.tile([P, 2, S], F32, name="above", tag="w2_raw")
+        fetch_y((0, 1), early_low)
+        for step in (raise_floor, lower_ceiling, squared):
+            step(0)
+            step(1)
+        c = [keep.tile([P, S], F32, name="c%d" % t) for t in range(PACK)]
+
+        def gained_c(t):
+            nc.scalar.activation(c[t][:], banks[4 + t][:], ACT.Copy, scale=gain[:, t : t + 1])
+
+        for t in range(PACK):
+            product(banks[4 + t][:], w2_q, t, xt)
+        gained_c(0)
+        gained_c(1)
+        fetch_y((2, 3), late_low)
+        stay_weight(0)
+        stay_weight(1)
+        raise_floor(2)
+        gained_c(2)
+        raise_floor(3)
+        for step in (lower_ceiling, squared):
+            step(2)
+            step(3)
+        move_weight(0)
+        move_weight(1)
+        gained_c(3)
+        stay_weight(2)
+        stay_weight(3)
+        move_weight(slice(2, 4))
 
         out_rows = out.rearrange("(p t) j -> p t j", t=PACK)
-        bank = 0
-        for i, (j0, n) in enumerate(CHUNKS):
+
+        def blend(i, part0, part1):
+            j0, n = CHUNKS[i]
             js = slice(j0, j0 + n)
+            for t0 in (0, 2):
+                for t in (t0, t0 + 1):
+                    nc.vector.tensor_tensor(part0[t], c[t][:].indirect(lists(v0_t, j0, n)), stay[:, t, js], ALU.mult)
+                for t in (t0, t0 + 1):
+                    nc.vector.tensor_tensor(part1[t], c[t][:].indirect(lists(v1_t, j0, n)), move[:, t, js], ALU.mult)
+
+        def add_parts(blocks, part0, part1):
             for t in range(PACK):
-                nc.vector.tensor_tensor(part0[:, t, js], c[t][:].indirect(lists(v0_t, j0, n)), stay[:, t, js], ALU.mult)
-                nc.vector.tensor_tensor(part1[:, t, js], c[t][:].indirect(lists(v1_t, j0, n)), move[:, t, js], ALU.mult)
-            z = keep.tile([P, n * PACK], BF16, name="z%d" % i, align_bytes=64)
-            nc.vector.tensor_tensor(
-                z[:].rearrange("p (c i t) -> p c t i", i=4, t=PACK),
-                part0[:, :, js].rearrange("p t (c i) -> p c t i", i=4),
-                part1[:, :, js].rearrange("p t (c i) -> p c t i", i=4),
-                ALU.add,
+                for k, b in enumerate(blocks):
+                    cols = slice(k * P, (k + 1) * P)
+                    total = banks[b % 2][:, t * P : (t + 1) * P]
+                    nc.tensor.matmul(total, part1[t][:, cols], ident[:], is_transpose=True, start=True, stop=False)
+                    nc.tensor.matmul(total, part0[t][:, cols], ident[:], is_transpose=True, start=False, stop=True)
+
+        def turn_back(b, back):
+            turned = keep.tile([P, 512], BF16, name="turned%d" % b)
+            nc.scalar.copy(
+                out=turned[:].rearrange("j (u p e) -> j u p e", u=2, e=2),
+                in_=banks[b % 2][:].rearrange("j (u e p) -> j u p e", u=2, e=2),
             )
-            z_q = quantize("z%d" % i, z[:], n)
-            res = keep.tile([P, PACK, n], F32, name="res%d" % i)
-            for t0 in range(0, PACK, 2):
-                for t in range(t0, t0 + 2):
-                    product(banks[bank][:, (t - t0) * n : (t - t0 + 1) * n], w3_q, t, z_q)
-                pair = res[:, t0 : t0 + 2, :].rearrange("p t j -> p (t j)")
-                if i == len(CHUNKS) - 1 and t0 == 2:
-                    nc.vector.tensor_copy(out=pair, in_=banks[bank][:, 0 : 2 * n])
+            for u in range(2):
+                nc.tensor.transpose(back[:, u * P : (u + 1) * P], turned[:].bitcast(F32)[:, u * P : (u + 1) * P], ident[:])
+
+        def lay_out(b, back):
+            z = keep.tile([P, P * PACK], BF16, name="z%d" % b, tag="z%d" % b, align_bytes=64)
+            nc.scalar.copy(
+                out=z[:].bitcast(F32).rearrange("p (j u) -> p j u", u=2),
+                in_=back[:, 0 : 2 * P].rearrange("p (u j) -> p j u", u=2),
+            )
+            return z
+
+        def finish(b, z, out_banks):
+            js = slice(b * P, (b + 1) * P)
+            z_q = quantize("z%d" % b, z[:], P)
+            res = keep.tile([P, PACK, P], F32, name="res%d" % b)
+            share = PACK // len(out_banks)
+            for k, bank in enumerate(out_banks):
+                t0 = k * share
+                for t in range(t0, t0 + share):
+                    product(bank[:, (t - t0) * P : (t - t0 + 1) * P], w3_q, t, z_q)
+                rows = res[:, t0 : t0 + share, :].rearrange("p t j -> p (t j)")
+                if k == 0:
+                    nc.scalar.copy(out=rows, in_=bank[:, 0 : share * P])
                 else:
-                    nc.scalar.copy(out=pair, in_=banks[bank][:, 0 : 2 * n])
-                nc.sync.dma_start(out=out_rows[:, t0 : t0 + 2, js], in_=res[:, t0 : t0 + 2, :])
-                bank = bank + 1
+                    nc.vector.tensor_copy(out=rows, in_=bank[:, 0 : share * P])
+                nc.sync.dma_start(out=out_rows[:, t0 : t0 + share, js], in_=res[:, t0 : t0 + share, :])
+
+        late = [part[:, 2:4, :].rearrange("p a (b j) -> p (a b) j", b=2) for part in (part0, part1)]
+        lead = keep.tile([P, 2, HALF], F32, name="lead", tag="lead", align_bytes=64)
+        first = [[lead[:, k, :]] + [part[:, t, :] for t in range(1, PACK)] for k, part in enumerate((part0, part1))]
+        second = [[part[:, t, :] for t in range(PACK)] for part in late]
+        blend(0, *first)
+        add_parts((0, 1), *first)
+        turn_back(0, banks[2])
+        turn_back(1, banks[3])
+        z0 = lay_out(0, banks[2])
+        z1 = lay_out(1, banks[3])
+        w3_q = quantize("w3", cast_weight("w3_bf", w3_raw, "lead")[:], 512)
+        blend(1, *second)
+        add_parts((2,), *second)
+        turn_back(2, banks[3])
+        z2 = lay_out(2, banks[3])
+        finish(0, z0, [banks[4]])
+        finish(1, z1, [banks[3]])
+        last0 = keep.tile([P, PACK, P], F32, name="last0", tag="z0", align_bytes=64)
+        last1 = keep.tile([P, PACK, P], F32, name="last1", tag="z1", align_bytes=64)
+        blend(2, *[[part[:, t, :] for t in range(PACK)] for part in (last0, last1)])
+        finish(2, z2, [banks[5]])
+        z3 = keep.tile([P, P * PACK], BF16, name="z3", tag="z2", align_bytes=64)
+        nc.vector.tensor_tensor(
+            z3[:].rearrange("p (c i t) -> p c t i", i=4, t=PACK),
+            last1[:].rearrange("p t (c i) -> p c t i", i=4),
+            last0[:].rearrange("p t (c i) -> p c t i", i=4),
+            ALU.add,
+        )
+        finish(3, z3, [banks[6], banks[7]])

@@ -65,7 +65,7 @@ def tile_picked_smstep_none_p_kernel(tc, x_words, x_scales, w1, w2, gn, w3, offs
             )
 
         xs = keep.tile([P, T], U8, name="xs", align_bytes=64)
-        nc.vector.memset(xs[:].bitcast(I32), 0)
+        nc.gpsimd.memset(xs[:].bitcast(I32), 0)
 
         offs_t = load_list("offs_t", offs)
         two_t = load_list("two_t", two)

from contextlib import ExitStack

import concourse.mybir as mybir
from concourse.masks import make_identity

K, T, S, N, H = 512, 2048, 512, 512, 512
FLOPS = 3 * 2 * 512 * 512 * 512

F32 = mybir.dt.float32
BF16 = mybir.dt.bfloat16
I32 = mybir.dt.int32
U32 = mybir.dt.uint32
U16 = mybir.dt.uint16
U8 = mybir.dt.uint8
FP8X4 = mybir.dt.float8_e4m3fn_x4
ALU = mybir.AluOpType
ACT = mybir.ActivationFunctionType

P = 128
PACK = 4
HALF = 256
CHUNKS = ((0, 256), (256, 128), (384, 128))


def tile_picked_smstep_none_p_kernel(tc, x_words, x_scales, w1, w2, gn, w3, offs, two, e1, e0, v0, v1, out):
    nc = tc.nc
    with ExitStack() as ctx:
        keep = ctx.enter_context(tc.tile_pool(name="keep", bufs=1))
        psum = ctx.enter_context(tc.psum_pool(name="psum", bufs=1))

        def load_list(name, src):
            tile = keep.tile([P, S // 16], U16, name=name)
            nc.sync.dma_start(tile[:], src)
            return tile

        def load_weight(name, w, c0=0, width=512):
            raw = keep.tile([P, PACK, width], F32, name=name, tag=name)
            nc.sync.dma_start(out=raw[:], in_=w.rearrange("(p j) c -> p j c", j=PACK)[:, :, c0 : c0 + width])
            return raw

        def cast_weight(name, raws, tag):
            grouped = keep.tile([P, PACK * P * PACK], BF16, name=name, tag=tag, align_bytes=64)
            dealt = grouped[:].rearrange("p (t m j) -> p m j t", t=PACK, j=PACK)
            step = P // len(raws)
            for i, raw in enumerate(raws):
                nc.scalar.copy(out=dealt[:, i * step : (i + 1) * step], in_=raw[:].rearrange("p j (m t) -> p m j t", t=PACK))
            return grouped

        def quantize(name, grouped, width):
            codes = keep.tile([P, width], U32, name=name + "_codes", align_bytes=64)
            scales = keep.tile([P, width], U8, name=name + "_scales", align_bytes=64)
            nc.vector.quantize_mx(out=codes[:].bitcast(FP8X4), scales=scales[:], in_=grouped)
            return codes, scales

        def product(acc, weight, t, moving, places=slice(None)):
            cols = slice(t * P, (t + 1) * P)
            nc.tensor.matmul_mx(
                out=acc,
                lhsT=weight[0][:, cols].bitcast(FP8X4),
                lhsT_scale=weight[1][:, cols],
                rhs=moving[0][:, places].bitcast(FP8X4),
                rhs_scale=moving[1][:, places],
                start=True,
                stop=True,
            )

        xs = keep.tile([P, T], U8, name="xs", align_bytes=64)
        nc.gpsimd.memset(xs[:].bitcast(I32), 0)

        offs_t = load_list("offs_t", offs)
        two_t = load_list("two_t", two)
        w1_raw = [load_weight("w1_raw0", w1, 0, 256)]
        for q in range(4):
            nc.sync.dma_start(out=xs[32 * q : 32 * q + 4, :].bitcast(I32), in_=x_scales[0][4 * q : 4 * q + 4, :].bitcast(I32))
        w1_raw.append(load_weight("w1_raw1", w1, 256, 256))
        xw = keep.tile([P, T], I32, name="xw", align_bytes=64)
        nc.sync.dma_start(out=xw[:], in_=x_words[0].rearrange("p n t -> p (n t)").bitcast(I32))
        e0_t = load_list("e0_t", e0)
        e1_t = load_list("e1_t", e1)
        w2_raw = load_weight("w2_raw", w2)
        gain = keep.tile([P, PACK], F32, name="gain")
        nc.sync.dma_start(out=gain[:], in_=gn.rearrange("(p t) o -> p (t o)", t=PACK))
        v0_t = load_list("v0_t", v0)
        v1_t = load_list("v1_t", v1)
        w3_raw = [load_weight("w3_raw%d" % i, w3, 256 * i, 256) for i in range(2)]

        banks = [psum.tile([P, 512], F32, name="bank%d" % b) for b in range(8)]

        def lists(lst, j0, n):
            return lst[:, j0 // 16 : (j0 + n) // 16]

        def pick_scales(name, lst):
            tile = keep.tile([P, S], U8, name=name, align_bytes=64)
            nc.vector.tensor_copy(tile[:], xs[:].indirect(lst[:]))
            return tile

        def pick_words(name, lst, n):
            tile = keep.tile([P, S], U32, name=name, align_bytes=64)
            for j0 in range(0, S, n):
                nc.vector.tensor_copy(tile[:, j0 : j0 + n], xw[:].bitcast(U32).indirect(lists(lst, j0, n)))
            return tile

        xq_scales = pick_scales("xq_scales", offs_t)
        xt_scales = pick_scales("xt_scales", two_t)
        w1_q = quantize("w1", cast_weight("w1_bf", w1_raw, "w1_bf")[:], 512)
        xq = (pick_words("xq_words", offs_t, HALF), xq_scales)
        xt = (pick_words("xt_words", two_t, S), xt_scales)

        ident = keep.tile([P, P], F32, name="ident")
        make_identity(nc, ident[:])

        early_low = keep.tile([P, 2, S], F32, name="early_low")
        diff = keep.tile([P, PACK, S], F32, name="diff")
        clip = keep.tile([P, PACK, S], F32, name="clip")
        square = keep.tile([P, PACK, S], F32, name="square")
        stay = keep.tile([P, PACK, S], F32, name="stay")
        move = keep.tile([P, PACK, S], F32, name="move")
        part0 = keep.tile([P, PACK, HALF], F32, name="part0")
        part1 = keep.tile([P, PACK, HALF], F32, name="part1")

        def fetch_y(tiles, low):
            for t in tiles:
                nc.vector.tensor_copy(low[:, t % 2, :], y[t][:].indirect(e0_t[:]))
            for t in tiles:
                nc.vector.tensor_tensor(diff[:, t, :], y[t][:].indirect(e1_t[:]), low[:, t % 2, :], ALU.subtract)

        def raise_floor(t):
            nc.scalar.activation(above[:, t % 2, :], diff[:, t, :], ACT.Relu, bias=1.0, scale=-1.0)

        def lower_ceiling(t):
            nc.scalar.activation(clip[:, t, :], above[:, t % 2, :], ACT.Relu, bias=2.0, scale=-1.0)

        def squared(t):
            nc.scalar.activation(square[:, t, :], clip[:, t, :], ACT.Square, bias=1.0, scale=-0.5)

        def stay_weight(ts):
            nc.vector.scalar_tensor_tensor(stay[:, ts, :], clip[:, ts, :], 1.0, square[:, ts, :], ALU.add, ALU.mult)

        def move_weight(ts):
            nc.scalar.activation(move[:, ts, :], stay[:, ts, :], ACT.Copy, bias=1.0, scale=-1.0)

        y = []
        for t in range(PACK):
            tile = keep.tile([P, 2 * S], F32, name="y%d" % t)
            y.append(tile)
        for h in range(2):
            places = slice(h * HALF, (h + 1) * HALF)
            for t in range(2):
                bank = banks[4 * h + t]
                product(bank[:, 0:HALF], w1_q, t, xq, places)
                nc.scalar.copy(out=y[t][:, places], in_=bank[:, 0:HALF])
        for t in range(2, PACK):
            product(banks[t][:], w1_q, t, xq)
            nc.scalar.copy(out=y[t][:, 0:S], in_=banks[t][:])
        w2_q = quantize("w2", cast_weight("w2_bf", [w2_raw], "w2_bf")[:], 512)

        late_low = keep.tile([P, 2, S], F32, name="late_low", tag="w2_bf", align_bytes=64)
        above = keep.tile([P, 2, S], F32, name="above", tag="w2_raw")
        fetch_y((0, 1), early_low)
        for step in (raise_floor, lower_ceiling, squared):
            step(0)
            step(1)
        c = [keep.tile([P, S], F32, name="c%d" % t) for t in range(PACK)]

        def gained_c(t):
            nc.scalar.activation(c[t][:], banks[4 + t][:], ACT.Copy, scale=gain[:, t : t + 1])

        for t in range(PACK):
            product(banks[4 + t][:], w2_q, t, xt)
        gained_c(0)
        gained_c(1)
        fetch_y((2, 3), late_low)
        stay_weight(0)
        stay_weight(1)
        raise_floor(2)
        gained_c(2)
        raise_floor(3)
        for step in (lower_ceiling, squared):
            step(2)
            step(3)
        move_weight(0)
        move_weight(1)
        gained_c(3)
        stay_weight(2)
        stay_weight(3)
        move_weight(slice(2, 4))

        out_rows = out.rearrange("(p t) j -> p t j", t=PACK)

        def blend(i, part0, part1):
            j0, n = CHUNKS[i]
            js = slice(j0, j0 + n)
            for t0 in (0, 2):
                for t in (t0, t0 + 1):
                    nc.vector.tensor_tensor(part0[t], c[t][:].indirect(lists(v0_t, j0, n)), stay[:, t, js], ALU.mult)
                for t in (t0, t0 + 1):
                    nc.vector.tensor_tensor(part1[t], c[t][:].indirect(lists(v1_t, j0, n)), move[:, t, js], ALU.mult)

        def add_parts(blocks, part0, part1):
            for t in range(PACK):
                for k, b in enumerate(blocks):
                    cols = slice(k * P, (k + 1) * P)
                    total = banks[b % 2][:, t * P : (t + 1) * P]
                    nc.tensor.matmul(total, part1[t][:, cols], ident[:], is_transpose=True, start=True, stop=False)
                    nc.tensor.matmul(total, part0[t][:, cols], ident[:], is_transpose=True, start=False, stop=True)

        def turn_back(b, back):
            turned = keep.tile([P, 512], BF16, name="turned%d" % b)
            nc.scalar.copy(
                out=turned[:].rearrange("j (u p e) -> j u p e", u=2, e=2),
                in_=banks[b % 2][:].rearrange("j (u e p) -> j u p e", u=2, e=2),
            )
            for u in range(2):
                nc.tensor.transpose(back[:, u * P : (u + 1) * P], turned[:].bitcast(F32)[:, u * P : (u + 1) * P], ident[:])

        def lay_out(b, back):
            z = keep.tile([P, P * PACK], BF16, name="z%d" % b, tag="z%d" % b, align_bytes=64)
            nc.scalar.copy(
                out=z[:].bitcast(F32).rearrange("p (j u) -> p j u", u=2),
                in_=back[:, 0 : 2 * P].rearrange("p (u j) -> p j u", u=2),
            )
            return z

        def finish(b, z, out_banks):
            js = slice(b * P, (b + 1) * P)
            z_q = quantize("z%d" % b, z[:], P)
            res = keep.tile([P, PACK, P], F32, name="res%d" % b)
            share = PACK // len(out_banks)
            for k, bank in enumerate(out_banks):
                t0 = k * share
                for t in range(t0, t0 + share):
                    product(bank[:, (t - t0) * P : (t - t0 + 1) * P], w3_q, t, z_q)
                rows = res[:, t0 : t0 + share, :].rearrange("p t j -> p (t j)")
                if k == 0:
                    nc.scalar.copy(out=rows, in_=bank[:, 0 : share * P])
                else:
                    nc.vector.tensor_copy(out=rows, in_=bank[:, 0 : share * P])
                nc.sync.dma_start(out=out_rows[:, t0 : t0 + share, js], in_=res[:, t0 : t0 + share, :])

        late = [part[:, 2:4, :].rearrange("p a (b j) -> p (a b) j", b=2) for part in (part0, part1)]
        lead = keep.tile([P, 2, HALF], F32, name="lead", tag="lead", align_bytes=64)
        first = [[lead[:, k, :]] + [part[:, t, :] for t in range(1, PACK)] for k, part in enumerate((part0, part1))]
        second = [[part[:, t, :] for t in range(PACK)] for part in late]
        blend(0, *first)
        add_parts((0, 1), *first)
        turn_back(0, banks[2])
        turn_back(1, banks[3])
        z0 = lay_out(0, banks[2])
        z1 = lay_out(1, banks[3])
        w3_q = quantize("w3", cast_weight("w3_bf", w3_raw, "lead")[:], 512)
        blend(1, *second)
        add_parts((2,), *second)
        turn_back(2, banks[3])
        z2 = lay_out(2, banks[3])
        finish(0, z0, [banks[4]])
        finish(1, z1, [banks[3]])
        last0 = keep.tile([P, PACK, P], F32, name="last0", tag="z0", align_bytes=64)
        last1 = keep.tile([P, PACK, P], F32, name="last1", tag="z1", align_bytes=64)
        blend(2, *[[part[:, t, :] for t in range(PACK)] for part in (last0, last1)])
        finish(2, z2, [banks[5]])
        z3 = keep.tile([P, P * PACK], BF16, name="z3", tag="z2", align_bytes=64)
        nc.vector.tensor_tensor(
            z3[:].rearrange("p (c i t) -> p c t i", i=4, t=PACK),
            last1[:].rearrange("p t (c i) -> p c t i", i=4),
            last0[:].rearrange("p t (c i) -> p c t i", i=4),
            ALU.add,
        )
        finish(3, z3, [banks[6], banks[7]])
